import numpy as np
import ml_dtypes


def mxq(x, axis, fmt="e4m3"):
    dtype, down = {"e4m3": (ml_dtypes.float8_e4m3fn, 7), "e5m2": (ml_dtypes.float8_e5m2, 14)}[fmt]
    v = np.moveaxis(np.asarray(x, np.float32).astype(ml_dtypes.bfloat16).astype(np.float64), axis, -1)
    blocks = v.reshape(v.shape[:-1] + (-1, 32))
    amax = np.abs(blocks).max(-1, keepdims=True)
    byte = np.maximum(np.where(amax > 0, np.frexp(amax)[1] - 1 + 127, 0) - down, 1)
    scale = np.exp2(byte - 127.0)
    codes = (blocks / scale).astype(np.float32).astype(dtype).astype(np.float64)
    return np.moveaxis((codes * scale).reshape(v.shape), -1, axis)


WIDE = False


def mx_kscale(k):
    if not WIDE:
        return np.ones(k)
    levels = np.array([24, -24, 12, -12, 0])
    if k % 512:
        return np.exp2(np.random.permutation(np.resize(levels, k // 32))).repeat(32)
    a = np.empty((k // 512, 16))
    for p in range(k // 512):
        a[p, :8] = np.random.permutation(np.resize(levels, 8))
        for g in range(8):
            far = levels[np.abs(levels - a[p, g]) >= 10]
            a[p, g + 8] = far[np.random.randint(len(far))]
    return np.exp2(a.ravel()).repeat(32)


def f64(x):
    return np.asarray(x).astype(np.float64)


def striped(idx):
    return np.tile(idx.reshape(-1, 16).T, (8, 1)).astype(np.uint16)


def unstriped(offs):
    return offs[:16].T.reshape(-1).astype(np.int64)


E2M1 = np.array([0.0, 0.5, 1.0, 1.5, 2.0, 3.0, 4.0, 6.0, -0.0, -0.5, -1.0, -1.5, -2.0, -3.0, -4.0, -6.0])


def pack_weight(w, fmt):
    k, n = w.shape
    w = f64(np.asarray(w, np.float32).astype(ml_dtypes.bfloat16)).reshape(k // 32, 32, n)
    amax = np.abs(w).max(1)
    if fmt == "e4m3":
        byte = np.frexp(amax)[1] - 1 + 127 - 7
    else:
        mant, ex = np.frexp(amax / 6.0)
        byte = np.where(mant > 0.5, ex, ex - 1) + 127
    byte = np.clip(np.where(amax > 0, byte, 1), 1, 254)
    scaled = (w * np.exp2(127.0 - byte)[:, None, :]).reshape(k, n).astype(np.float32)
    by_word = np.ascontiguousarray(scaled.reshape(k // 512, 128, 4, n).transpose(0, 1, 3, 2))
    if fmt == "e4m3":
        words = by_word.astype(ml_dtypes.float8_e4m3fn).view(np.uint8)
    else:
        c = by_word.astype(ml_dtypes.float4_e2m1fn).view(np.uint8) & 0xF
        words = (c[..., 0::2] | (c[..., 1::2] << 4)).reshape(k // 512, 128, 2 * n)
    return np.ascontiguousarray(words), np.ascontiguousarray(byte.astype(np.uint8).reshape(k // 512, 16, n))


def unpack_weight(words, scales, fmt):
    g, _, n = scales.shape
    words = np.ascontiguousarray(words).reshape(g, 128, n, -1)
    if fmt == "e4m3":
        vals = words.view(ml_dtypes.float8_e4m3fn).astype(np.float64)
    else:
        nib = np.empty((g, 128, n, 4), np.uint8)
        nib[..., 0::2] = words & 0xF
        nib[..., 1::2] = words >> 4
        vals = E2M1[nib]
    vals = vals * np.repeat(np.exp2(scales.astype(np.float64) - 127.0), 8, axis=1)[..., None]
    return vals.transpose(0, 1, 3, 2).reshape(g * 512, n)


def sigm(f):
    return 1.0 / (1.0 + np.exp(-np.maximum(f, -700.0)))


K, N, T, J = 512, 256, 1024, 512


def setup_inputs():
    n = np.random.standard_normal
    s = mx_kscale(K)[:, None]
    p_tab = pack_weight(n((K, T)) * s, "e4m3")
    p_wh4 = pack_weight(n((K, N)) / np.sqrt(K) / s, "e2m1")
    return {
        "tab_words": p_tab[0],
        "tab_scales": p_tab[1],
        "wg": (n((K, N)) / np.sqrt(K) / s).astype(np.float32),
        "wh4_words": p_wh4[0],
        "wh4_scales": p_wh4[1],
        "whd": (0.4 * (n((K, N)) / np.sqrt(K) / s)).astype(np.float32),
        "bg": (0.3 * n(N) - 1.0).astype(np.float32),
        "rT": (n((N, T))).astype(np.float32),
        "offs": striped(np.random.permutation(T)[:J]),
    }


def reference(tab_words, tab_scales, wg, wh4_words, wh4_scales, whd, bg, rT, offs):
    idx = unstriped(offs)
    tab_ = unpack_weight(tab_words, tab_scales, "e4m3")[:, idx]
    wg_ = mxq(f64(wg), 0, "e4m3")
    wh4_ = unpack_weight(wh4_words, wh4_scales, "e2m1")
    whd_ = mxq(f64(whd), 0, "e4m3")
    ga = wg_.T @ tab_
    gate = sigm(ga + f64(bg)[:, None])
    ha = wh4_.T @ tab_ + whd_.T @ tab_
    return f64(rT)[:, idx] + gate * (np.tanh(ha) - f64(rT)[:, idx])

@@ -1,0 +1,155 @@
+from contextlib import ExitStack
+
+import concourse.mybir as mybir
+
+K, N, T, J = 512, 256, 1024, 512
+FLOPS = 3 * 2 * K * N * J
+
+F32 = mybir.dt.float32
+BF16 = mybir.dt.bfloat16
+I32 = mybir.dt.int32
+U32 = mybir.dt.uint32
+U16 = mybir.dt.uint16
+U8 = mybir.dt.uint8
+FP8X4 = mybir.dt.float8_e4m3fn_x4
+FP4X4 = mybir.dt.float4_e2m1fn_x4
+ALU = mybir.AluOpType
+ACT = mybir.ActivationFunctionType
+
+P = 128
+PACK = 4
+HALVES = N // P
+
+
+def tile_list_hwayt_dl_tanh_kernel(
+    tc, tab_words, tab_scales, wg, wh4_words, wh4_scales, whd, bg, rT, offs, out
+):
+    nc = tc.nc
+    with ExitStack() as ctx:
+        lists = ctx.enter_context(tc.tile_pool(name="lists", bufs=1))
+        keep = ctx.enter_context(tc.tile_pool(name="keep", bufs=1))
+        psum = ctx.enter_context(tc.psum_pool(name="psum", bufs=1))
+
+        offsets = lists.tile([P, J // 16], U16, name="offsets")
+        nc.sync.dma_start(offsets[:], offs)
+
+        tab_s = keep.tile([P, T // 4], I32, name="tab_s", align_bytes=64)
+        nc.vector.memset(tab_s[:], 0)
+        tab_s_rows = tab_scales[0].bitcast(I32)
+        for q in range(4):
+            nc.scalar.dma_start(tab_s[32 * q : 32 * q + 4, :], tab_s_rows[4 * q : 4 * q + 4, :])
+
+        warm_in = keep.tile([P, 1], F32, name="warm_in", tag="slot_a", align_bytes=64)
+        warm_out = keep.tile([P, 1], F32, name="warm_out", tag="slot_b", align_bytes=64)
+        nc.vector.memset(warm_in[:], 0.0)
+        nc.scalar.activation(warm_out[:], warm_in[:], ACT.Sigmoid)
+
+        tab_w = keep.tile([P, T], I32, name="tab_w", align_bytes=64)
+        nc.sync.dma_start(tab_w[:], tab_words[0].rearrange("p t i -> p (t i)").bitcast(I32))
+        wg_raw = keep.tile([P, PACK, N], F32, name="wg_raw", tag="slot_c", align_bytes=64)
+        nc.sync.dma_start(wg_raw[:], wg.rearrange("(p i) n -> p i n", i=PACK))
+        whd_raw = keep.tile([P, PACK, N], F32, name="whd_raw", align_bytes=64)
+        nc.sync.dma_start(whd_raw[:], whd.rearrange("(p i) n -> p i n", i=PACK))
+
+        bias = keep.tile([P, HALVES], F32, name="bias")
+        with nc.allow_non_contiguous_dma(reason="one bias value a partition"):
+            nc.gpsimd.dma_start(bias[:], bg.rearrange("(h p) -> p h", p=P))
+        wh4_s = keep.tile([P, N // 4], I32, name="wh4_s", align_bytes=64)
+        nc.gpsimd.memset(wh4_s[:], 0)
+        wh4_s_rows = wh4_scales[0].bitcast(I32)
+        for q in range(4):
+            nc.gpsimd.dma_start(wh4_s[32 * q : 32 * q + 4, :], wh4_s_rows[4 * q : 4 * q + 4, :])
+        neg_bias = keep.tile([P, HALVES], F32, name="neg_bias")
+        nc.gpsimd.tensor_scalar(neg_bias[:], bias[:], -1.0, 0.0, ALU.mult, ALU.add)
+
+        wh4_w = keep.tile([P, N // 2], I32, name="wh4_w", tag="slot_a", align_bytes=64)
+        nc.sync.dma_start(wh4_w[:], wh4_words[0].bitcast(I32))
+        r_rows = []
+        r0 = keep.tile([P, T], F32, name="r0", tag="slot_b", align_bytes=64)
+        nc.sync.dma_start(r0[:], rT[0:P, :])
+        r_rows.append(r0)
+
+        v_w = keep.tile([P, J], U32, name="v_w", align_bytes=64)
+        nc.vector.tensor_copy(v_w[:], tab_w[:].bitcast(U32).indirect(offsets[:]))
+        v_s = keep.tile([P, J], U8, name="v_s", align_bytes=64)
+        nc.vector.tensor_copy(v_s[:], tab_s[:].bitcast(U8).indirect(offsets[:]))
+
+        def interleave(engine_copy, raw, h, name, tag):
+            grouped = keep.tile([P, P, PACK], BF16, name=name, tag=tag, align_bytes=64)
+            engine_copy(
+                grouped[:].rearrange("p (c e) i -> p c i e", e=4),
+                raw[:, :, h * P : (h + 1) * P].rearrange("p i (c e) -> p c i e", e=4),
+            )
+            return grouped
+
+        def quantise(grouped, name):
+            codes = keep.tile([P, P], U32, name=name + "_codes", align_bytes=64)
+            scales = keep.tile([P, P], U8, name=name + "_scales", align_bytes=64)
+            nc.vector.quantize_mx(
+                out=codes[:].bitcast(FP8X4),
+                scales=scales[:],
+                in_=grouped[:].rearrange("p n i -> p (n i)"),
+            )
+            return codes, scales
+
+        g0 = interleave(nc.scalar.copy, wg_raw, 0, "wg_g0", "wg_g0")
+        g1 = interleave(nc.scalar.copy, wg_raw, 1, "wg_g1", "wg_g1")
+        r1 = keep.tile([P, T], F32, name="r1", tag="slot_c", align_bytes=64)
+        nc.sync.dma_start(r1[:], rT[P : 2 * P, :])
+        r_rows.append(r1)
+        d1 = interleave(nc.scalar.copy, whd_raw, 1, "whd_g1", "whd_g1")
+        wg_q = [quantise(g0, "wg0")]
+        d0 = interleave(nc.vector.tensor_copy, whd_raw, 0, "whd_g0", "whd_g0")
+        wg_q.append(quantise(g1, "wg1"))
+        whd_q = [quantise(d0, "whd0"), quantise(d1, "whd1")]
+
+        carry, cand = [], []
+        for h in range(HALVES):
+            ga = psum.tile([P, J], F32, name="ga%d" % h)
+            ha = psum.tile([P, J], F32, name="ha%d" % h)
+            nc.tensor.matmul_mx(
+                out=ga[:], lhsT=wg_q[h][0][:].bitcast(FP8X4), lhsT_scale=wg_q[h][1][:],
+                rhs=v_w[:].bitcast(FP8X4), rhs_scale=v_s[:], start=True, stop=True,
+            )
+            nc.tensor.matmul_mx(
+                out=ha[:],
+                lhsT=wh4_w[:].bitcast(U8)[:, 2 * h * P : 2 * (h + 1) * P].bitcast(FP4X4),
+                lhsT_scale=wh4_s[:].bitcast(U8)[:, h * P : (h + 1) * P],
+                rhs=v_w[:].bitcast(FP8X4), rhs_scale=v_s[:], start=True, stop=False,
+            )
+            nc.tensor.matmul_mx(
+                out=ha[:], lhsT=whd_q[h][0][:].bitcast(FP8X4), lhsT_scale=whd_q[h][1][:],
+                rhs=v_w[:].bitcast(FP8X4), rhs_scale=v_s[:], start=False, stop=True,
+            )
+            c_h = keep.tile([P, J], F32, name="carry%d" % h)
+            nc.scalar.activation(c_h[:], ga[:], ACT.Sigmoid, bias=neg_bias[:, h : h + 1], scale=-1.0)
+            t_h = keep.tile([P, J], F32, name="cand%d" % h)
+            nc.scalar.activation(t_h[:], ha[:], ACT.Tanh)
+            carry.append(c_h)
+            cand.append(t_h)
+
+        kept = [keep.tile([P, J], F32, name="kept%d" % h) for h in range(HALVES)]
+        made = [keep.tile([P, J], F32, name="made%d" % h) for h in range(HALVES)]
+        res = [keep.tile([P, J], F32, name="res%d" % h) for h in range(HALVES)]
+
+        def keep_part(h):
+            nc.vector.tensor_tensor(kept[h][:], r_rows[h][:].indirect(offsets[:]), carry[h][:], ALU.mult)
+
+        def made_part(h, cols):
+            nc.vector.scalar_tensor_tensor(
+                made[h][:, cols], carry[h][:, cols], -1.0, cand[h][:, cols], ALU.add, ALU.mult
+            )
+
+        def finish(h, cols):
+            nc.vector.tensor_tensor(res[h][:, cols], kept[h][:, cols], made[h][:, cols], ALU.subtract)
+            nc.sync.dma_start(out[h * P : (h + 1) * P, cols], res[h][:, cols])
+
+        whole, left, right = slice(0, J), slice(0, J // 2), slice(J // 2, J)
+        keep_part(0)
+        made_part(0, whole)
+        keep_part(1)
+        finish(0, whole)
+        made_part(1, left)
+        made_part(1, right)
+        finish(1, left)
+        finish(1, right)

@@ -33,46 +33,47 @@ def tile_list_hwayt_dl_tanh_kernel(
         offsets = lists.tile([P, J // 16], U16, name="offsets")
         nc.sync.dma_start(offsets[:], offs)
 
+        wg_raw = keep.tile([P, PACK, N], F32, name="wg_raw", align_bytes=64)
+        nc.sync.dma_start(wg_raw[:], wg.rearrange("(p i) n -> p i n", i=PACK))
+
         tab_s = keep.tile([P, T // 4], I32, name="tab_s", align_bytes=64)
         nc.vector.memset(tab_s[:], 0)
         tab_s_rows = tab_scales[0].bitcast(I32)
         for q in range(4):
             nc.scalar.dma_start(tab_s[32 * q : 32 * q + 4, :], tab_s_rows[4 * q : 4 * q + 4, :])
 
-        warm_in = keep.tile([P, 1], F32, name="warm_in", tag="slot_a", align_bytes=64)
-        warm_out = keep.tile([P, 1], F32, name="warm_out", tag="slot_b", align_bytes=64)
-        nc.vector.memset(warm_in[:], 0.0)
-        nc.scalar.activation(warm_out[:], warm_in[:], ACT.Sigmoid)
-
         tab_w = keep.tile([P, T], I32, name="tab_w", align_bytes=64)
         nc.sync.dma_start(tab_w[:], tab_words[0].rearrange("p t i -> p (t i)").bitcast(I32))
-        wg_raw = keep.tile([P, PACK, N], F32, name="wg_raw", tag="slot_c", align_bytes=64)
-        nc.sync.dma_start(wg_raw[:], wg.rearrange("(p i) n -> p i n", i=PACK))
         whd_raw = keep.tile([P, PACK, N], F32, name="whd_raw", align_bytes=64)
         nc.sync.dma_start(whd_raw[:], whd.rearrange("(p i) n -> p i n", i=PACK))
+        r_rows = [keep.tile([P, T], F32, name="r%d" % h, tag="r%d" % h, align_bytes=64) for h in range(HALVES)]
+        for h in range(HALVES):
+            nc.sync.dma_start(r_rows[h][:], rT[h * P : (h + 1) * P, :])
 
-        bias = keep.tile([P, HALVES], F32, name="bias")
-        with nc.allow_non_contiguous_dma(reason="one bias value a partition"):
-            nc.gpsimd.dma_start(bias[:], bg.rearrange("(h p) -> p h", p=P))
         wh4_s = keep.tile([P, N // 4], I32, name="wh4_s", align_bytes=64)
         nc.gpsimd.memset(wh4_s[:], 0)
         wh4_s_rows = wh4_scales[0].bitcast(I32)
         for q in range(4):
             nc.gpsimd.dma_start(wh4_s[32 * q : 32 * q + 4, :], wh4_s_rows[4 * q : 4 * q + 4, :])
+
+        warm_in = keep.tile([P, 1], F32, name="warm_in")
+        warm_out = keep.tile([P, 1], F32, name="warm_out")
+        nc.vector.memset(warm_in[:], 0.0)
+        nc.scalar.activation(warm_out[:], warm_in[:], ACT.Sigmoid)
+        bias = keep.tile([P, HALVES], F32, name="bias")
+        with nc.allow_non_contiguous_dma(reason="one bias value a partition"):
+            nc.scalar.dma_start(bias[:], bg.rearrange("(h p) -> p h", p=P))
         neg_bias = keep.tile([P, HALVES], F32, name="neg_bias")
-        nc.gpsimd.tensor_scalar(neg_bias[:], bias[:], -1.0, 0.0, ALU.mult, ALU.add)
+        wh4_w = keep.tile([P, N // 2], I32, name="wh4_w", align_bytes=64)
 
-        wh4_w = keep.tile([P, N // 2], I32, name="wh4_w", tag="slot_a", align_bytes=64)
-        nc.sync.dma_start(wh4_w[:], wh4_words[0].bitcast(I32))
-        r_rows = []
-        r0 = keep.tile([P, T], F32, name="r0", tag="slot_b", align_bytes=64)
-        nc.sync.dma_start(r0[:], rT[0:P, :])
-        r_rows.append(r0)
-
-        v_w = keep.tile([P, J], U32, name="v_w", align_bytes=64)
-        nc.vector.tensor_copy(v_w[:], tab_w[:].bitcast(U32).indirect(offsets[:]))
         v_s = keep.tile([P, J], U8, name="v_s", align_bytes=64)
-        nc.vector.tensor_copy(v_s[:], tab_s[:].bitcast(U8).indirect(offsets[:]))
+        whole, left, right = slice(0, J), slice(0, J // 2), slice(J // 2, J)
+
+        def entries(cols):
+            return offsets[:, cols.start // 16 : cols.stop // 16]
+
+        def gather_words(cols):
+            nc.vector.tensor_copy(v_w[:, cols], tab_w[:].bitcast(U32).indirect(entries(cols)))
 
         def interleave(engine_copy, raw, h, name, tag):
             grouped = keep.tile([P, P, PACK], BF16, name=name, tag=tag, align_bytes=64)
@@ -82,58 +83,46 @@ def tile_list_hwayt_dl_tanh_kernel(
             )
             return grouped
 
-        def quantise(grouped, name):
-            codes = keep.tile([P, P], U32, name=name + "_codes", align_bytes=64)
+        def quantise(grouped, name, tag):
+            codes = keep.tile([P, P], U32, name=name + "_codes", tag=tag, align_bytes=64)
             scales = keep.tile([P, P], U8, name=name + "_scales", align_bytes=64)
             nc.vector.quantize_mx(
                 out=codes[:].bitcast(FP8X4),
                 scales=scales[:],
                 in_=grouped[:].rearrange("p n i -> p (n i)"),
             )
-            return codes, scales
+            return codes[:].bitcast(FP8X4), scales[:]
 
-        g0 = interleave(nc.scalar.copy, wg_raw, 0, "wg_g0", "wg_g0")
-        g1 = interleave(nc.scalar.copy, wg_raw, 1, "wg_g1", "wg_g1")
-        r1 = keep.tile([P, T], F32, name="r1", tag="slot_c", align_bytes=64)
-        nc.sync.dma_start(r1[:], rT[P : 2 * P, :])
-        r_rows.append(r1)
-        d1 = interleave(nc.scalar.copy, whd_raw, 1, "whd_g1", "whd_g1")
-        wg_q = [quantise(g0, "wg0")]
-        d0 = interleave(nc.vector.tensor_copy, whd_raw, 0, "whd_g0", "whd_g0")
-        wg_q.append(quantise(g1, "wg1"))
-        whd_q = [quantise(d0, "whd0"), quantise(d1, "whd1")]
+        def product(acc, weights, cols, start, stop):
+            nc.tensor.matmul_mx(
+                out=acc, lhsT=weights[0], lhsT_scale=weights[1],
+                rhs=v_w[:, cols].bitcast(FP8X4), rhs_scale=v_s[:, cols], start=start, stop=stop,
+            )
 
-        carry, cand = [], []
-        for h in range(HALVES):
-            ga = psum.tile([P, J], F32, name="ga%d" % h)
-            ha = psum.tile([P, J], F32, name="ha%d" % h)
-            nc.tensor.matmul_mx(
-                out=ga[:], lhsT=wg_q[h][0][:].bitcast(FP8X4), lhsT_scale=wg_q[h][1][:],
-                rhs=v_w[:].bitcast(FP8X4), rhs_scale=v_s[:], start=True, stop=True,
+        def wh4_half(h):
+            return (
+                wh4_w[:].bitcast(U8)[:, 2 * h * P : 2 * (h + 1) * P].bitcast(FP4X4),
+                wh4_s[:].bitcast(U8)[:, h * P : (h + 1) * P],
             )
-            nc.tensor.matmul_mx(
-                out=ha[:],
-                lhsT=wh4_w[:].bitcast(U8)[:, 2 * h * P : 2 * (h + 1) * P].bitcast(FP4X4),
-                lhsT_scale=wh4_s[:].bitcast(U8)[:, h * P : (h + 1) * P],
-                rhs=v_w[:].bitcast(FP8X4), rhs_scale=v_s[:], start=True, stop=False,
-            )
-            nc.tensor.matmul_mx(
-                out=ha[:], lhsT=whd_q[h][0][:].bitcast(FP8X4), lhsT_scale=whd_q[h][1][:],
-                rhs=v_w[:].bitcast(FP8X4), rhs_scale=v_s[:], start=False, stop=True,
-            )
-            c_h = keep.tile([P, J], F32, name="carry%d" % h)
-            nc.scalar.activation(c_h[:], ga[:], ACT.Sigmoid, bias=neg_bias[:, h : h + 1], scale=-1.0)
-            t_h = keep.tile([P, J], F32, name="cand%d" % h)
-            nc.scalar.activation(t_h[:], ha[:], ACT.Tanh)
-            carry.append(c_h)
-            cand.append(t_h)
 
+        carry = [keep.tile([P, J], F32, name="carry%d" % h) for h in range(HALVES)]
+        cand = [keep.tile([P, J], F32, name="cand%d" % h) for h in range(HALVES)]
         kept = [keep.tile([P, J], F32, name="kept%d" % h) for h in range(HALVES)]
-        made = [keep.tile([P, J], F32, name="made%d" % h) for h in range(HALVES)]
         res = [keep.tile([P, J], F32, name="res%d" % h) for h in range(HALVES)]
 
-        def keep_part(h):
-            nc.vector.tensor_tensor(kept[h][:], r_rows[h][:].indirect(offsets[:]), carry[h][:], ALU.mult)
+        def gate(h, weights, cols):
+            ga = psum.tile([P, cols.stop - cols.start], F32, name="ga%d_%d" % (h, cols.start))
+            product(ga[:], weights, cols, True, True)
+            nc.scalar.activation(carry[h][:, cols], ga[:], ACT.Sigmoid, bias=neg_bias[:, h : h + 1], scale=-1.0)
+
+        def candidate(h, weights):
+            ha = psum.tile([P, J], F32, name="ha%d" % h)
+            product(ha[:], weights, whole, True, False)
+            product(ha[:], wh4_half(h), whole, False, True)
+            nc.scalar.activation(cand[h][:], ha[:], ACT.Tanh)
+
+        def keep_part(h, cols):
+            nc.vector.tensor_tensor(kept[h][:, cols], r_rows[h][:].indirect(entries(cols)), carry[h][:, cols], ALU.mult)
 
         def made_part(h, cols):
             nc.vector.scalar_tensor_tensor(
@@ -144,12 +133,31 @@ def tile_list_hwayt_dl_tanh_kernel(
             nc.vector.tensor_tensor(res[h][:, cols], kept[h][:, cols], made[h][:, cols], ALU.subtract)
             nc.sync.dma_start(out[h * P : (h + 1) * P, cols], res[h][:, cols])
 
-        whole, left, right = slice(0, J), slice(0, J // 2), slice(J // 2, J)
-        keep_part(0)
+        nc.vector.tensor_copy(v_s[:], tab_s[:].bitcast(U8).indirect(offsets[:]))
+        g0 = interleave(nc.scalar.copy, wg_raw, 0, "wg_g0", "wg_g0")
+        g1 = interleave(nc.scalar.copy, wg_raw, 1, "wg_g1", "wg_g1")
+        nc.scalar.dma_start(wh4_w[:], wh4_words[0].bitcast(I32))
+        wg0 = quantise(g0, "wg0", "wg0_codes")
+        v_w = keep.tile([P, J], U32, name="v_w", align_bytes=64)
+        gather_words(left)
+        gather_words(right)
+        wg1 = quantise(g1, "wg1", "wg1_codes")
+        d0 = interleave(nc.vector.tensor_copy, whd_raw, 0, "whd_g0", "whd_g0")
+        d1 = interleave(nc.scalar.copy, whd_raw, 1, "whd_g1", "whd_g1")
+        nc.scalar.mul(neg_bias[:], bias[:], -1.0)
+        gate(0, wg0, left)
+        gate(0, wg0, right)
+        gate(1, wg1, whole)
+        whd1 = quantise(d1, "whd1", "whd1_codes")
+        whd0 = quantise(d0, "whd0", "whd0_codes")
+        candidate(0, whd0)
+        candidate(1, whd1)
+        keep_part(0, whole)
+        keep_part(1, whole)
+        made = [keep.tile([P, J], F32, name="made%d" % h) for h in range(HALVES)]
         made_part(0, whole)
-        keep_part(1)
-        finish(0, whole)
         made_part(1, left)
+        finish(0, whole)
         made_part(1, right)
         finish(1, left)
         finish(1, right)

@@ -30,42 +30,41 @@ def tile_list_hwayt_dl_tanh_kernel(
         keep = ctx.enter_context(tc.tile_pool(name="keep", bufs=1))
         psum = ctx.enter_context(tc.psum_pool(name="psum", bufs=1))
 
-        offsets = lists.tile([P, J // 16], U16, name="offsets")
-        nc.sync.dma_start(offsets[:], offs)
-
-        wg_raw = keep.tile([P, PACK, N], F32, name="wg_raw", align_bytes=64)
-        nc.sync.dma_start(wg_raw[:], wg.rearrange("(p i) n -> p i n", i=PACK))
-
-        tab_s = keep.tile([P, T // 4], I32, name="tab_s", align_bytes=64)
-        nc.vector.memset(tab_s[:], 0)
-        tab_s_rows = tab_scales[0].bitcast(I32)
-        for q in range(4):
-            nc.scalar.dma_start(tab_s[32 * q : 32 * q + 4, :], tab_s_rows[4 * q : 4 * q + 4, :])
 
         tab_w = keep.tile([P, T], I32, name="tab_w", align_bytes=64)
         nc.sync.dma_start(tab_w[:], tab_words[0].rearrange("p t i -> p (t i)").bitcast(I32))
+        offsets = lists.tile([P, J // 16], U16, name="offsets")
+        nc.sync.dma_start(offsets[:], offs)
+
+        def load_scale_rows(name, rows):
+            plane = keep.tile([P, rows.shape[1]], I32, name=name, align_bytes=64)
+            nc.vector.memset(plane[:], 0)
+            for q in range(4):
+                nc.sync.dma_start(plane[32 * q : 32 * q + 4, :], rows[4 * q : 4 * q + 4, :])
+            return plane
+
+        tab_s = load_scale_rows("tab_s", tab_scales[0].bitcast(I32))
+        wg_raw = keep.tile([P, PACK, N], F32, name="wg_raw", align_bytes=64)
+        nc.sync.dma_start(wg_raw[:], wg.rearrange("(p i) n -> p i n", i=PACK))
         whd_raw = keep.tile([P, PACK, N], F32, name="whd_raw", align_bytes=64)
         nc.sync.dma_start(whd_raw[:], whd.rearrange("(p i) n -> p i n", i=PACK))
-        r_rows = [keep.tile([P, T], F32, name="r%d" % h, tag="r%d" % h, align_bytes=64) for h in range(HALVES)]
-        for h in range(HALVES):
-            nc.sync.dma_start(r_rows[h][:], rT[h * P : (h + 1) * P, :])
-
-        wh4_s = keep.tile([P, N // 4], I32, name="wh4_s", align_bytes=64)
-        nc.gpsimd.memset(wh4_s[:], 0)
-        wh4_s_rows = wh4_scales[0].bitcast(I32)
-        for q in range(4):
-            nc.gpsimd.dma_start(wh4_s[32 * q : 32 * q + 4, :], wh4_s_rows[4 * q : 4 * q + 4, :])
+        bias = keep.tile([P, HALVES], F32, name="bias")
+        with nc.allow_non_contiguous_dma(reason="one bias value a partition"):
+            nc.sync.dma_start(bias[:], bg.rearrange("(h p) -> p h", p=P))
+        r_rows = [keep.tile([P, T], F32, name="r%d" % h, align_bytes=64) for h in range(HALVES)]
+        nc.sync.dma_start(r_rows[0][:], rT[0:P, :])
+        wh4_s = load_scale_rows("wh4_s", wh4_scales[0].bitcast(I32))
+        nc.sync.dma_start(r_rows[1][:], rT[P : 2 * P, :])
+        wh4_w = keep.tile([P, N // 2], I32, name="wh4_w", align_bytes=64)
+        nc.sync.dma_start(wh4_w[:], wh4_words[0].bitcast(I32))
 
         warm_in = keep.tile([P, 1], F32, name="warm_in")
         warm_out = keep.tile([P, 1], F32, name="warm_out")
         nc.vector.memset(warm_in[:], 0.0)
         nc.scalar.activation(warm_out[:], warm_in[:], ACT.Sigmoid)
-        bias = keep.tile([P, HALVES], F32, name="bias")
-        with nc.allow_non_contiguous_dma(reason="one bias value a partition"):
-            nc.scalar.dma_start(bias[:], bg.rearrange("(h p) -> p h", p=P))
         neg_bias = keep.tile([P, HALVES], F32, name="neg_bias")
-        wh4_w = keep.tile([P, N // 2], I32, name="wh4_w", align_bytes=64)
 
+        v_w = keep.tile([P, J], U32, name="v_w", align_bytes=64)
         v_s = keep.tile([P, J], U8, name="v_s", align_bytes=64)
         whole, left, right = slice(0, J), slice(0, J // 2), slice(J // 2, J)
 
@@ -133,26 +132,24 @@ def tile_list_hwayt_dl_tanh_kernel(
             nc.vector.tensor_tensor(res[h][:, cols], kept[h][:, cols], made[h][:, cols], ALU.subtract)
             nc.sync.dma_start(out[h * P : (h + 1) * P, cols], res[h][:, cols])
 
+        gather_words(whole)
         nc.vector.tensor_copy(v_s[:], tab_s[:].bitcast(U8).indirect(offsets[:]))
         g0 = interleave(nc.scalar.copy, wg_raw, 0, "wg_g0", "wg_g0")
         g1 = interleave(nc.scalar.copy, wg_raw, 1, "wg_g1", "wg_g1")
-        nc.scalar.dma_start(wh4_w[:], wh4_words[0].bitcast(I32))
-        wg0 = quantise(g0, "wg0", "wg0_codes")
-        v_w = keep.tile([P, J], U32, name="v_w", align_bytes=64)
-        gather_words(left)
-        gather_words(right)
-        wg1 = quantise(g1, "wg1", "wg1_codes")
-        d0 = interleave(nc.vector.tensor_copy, whd_raw, 0, "whd_g0", "whd_g0")
         d1 = interleave(nc.scalar.copy, whd_raw, 1, "whd_g1", "whd_g1")
         nc.scalar.mul(neg_bias[:], bias[:], -1.0)
+        wg0 = quantise(g0, "wg0", "wg0_codes")
+        wg1 = quantise(g1, "wg1", "wg1_codes")
+        d0 = interleave(nc.vector.tensor_copy, whd_raw, 0, "whd_g0", "whd_g0")
+        whd1 = quantise(d1, "whd1", "whd1_codes")
+        whd0 = quantise(d0, "whd0", "whd0_codes")
         gate(0, wg0, left)
         gate(0, wg0, right)
         gate(1, wg1, whole)
-        whd1 = quantise(d1, "whd1", "whd1_codes")
-        whd0 = quantise(d0, "whd0", "whd0_codes")
         candidate(0, whd0)
         candidate(1, whd1)
-        keep_part(0, whole)
+        keep_part(0, left)
+        keep_part(0, right)
         keep_part(1, whole)
         made = [keep.tile([P, J], F32, name="made%d" % h) for h in range(HALVES)]
         made_part(0, whole)

@@ -143,18 +143,18 @@ def tile_list_hwayt_dl_tanh_kernel(
         d0 = interleave(nc.vector.tensor_copy, whd_raw, 0, "whd_g0", "whd_g0")
         whd1 = quantise(d1, "whd1", "whd1_codes")
         whd0 = quantise(d0, "whd0", "whd0_codes")
-        gate(0, wg0, left)
-        gate(0, wg0, right)
+        first_pieces = [slice(0, J // 4), slice(J // 4, J // 2), right]
+        for cols in first_pieces:
+            gate(0, wg0, cols)
         gate(1, wg1, whole)
         candidate(0, whd0)
         candidate(1, whd1)
-        keep_part(0, left)
-        keep_part(0, right)
+        for cols in first_pieces:
+            keep_part(0, cols)
         keep_part(1, whole)
         made = [keep.tile([P, J], F32, name="made%d" % h) for h in range(HALVES)]
-        made_part(0, whole)
-        made_part(1, left)
-        finish(0, whole)
-        made_part(1, right)
-        finish(1, left)
-        finish(1, right)
+        for h in range(HALVES):
+            made_part(h, left)
+            made_part(h, right)
+            finish(h, left)
+            finish(h, right)

@@ -19,6 +19,7 @@ ACT = mybir.ActivationFunctionType
 P = 128
 PACK = 4
 HALVES = N // P
+EARLY = 384
 
 
 def tile_list_hwayt_dl_tanh_kernel(
@@ -44,7 +45,7 @@ def tile_list_hwayt_dl_tanh_kernel(
             return plane
 
         tab_s = load_scale_rows("tab_s", tab_scales[0].bitcast(I32))
-        wg_raw = keep.tile([P, PACK, N], F32, name="wg_raw", align_bytes=64)
+        wg_raw = keep.tile([P, PACK, N], F32, name="wg_raw", tag="wg_raw", align_bytes=64)
         nc.sync.dma_start(wg_raw[:], wg.rearrange("(p i) n -> p i n", i=PACK))
         whd_raw = keep.tile([P, PACK, N], F32, name="whd_raw", align_bytes=64)
         nc.sync.dma_start(whd_raw[:], whd.rearrange("(p i) n -> p i n", i=PACK))
@@ -65,7 +66,7 @@ def tile_list_hwayt_dl_tanh_kernel(
         neg_bias = keep.tile([P, HALVES], F32, name="neg_bias")
 
         v_w = keep.tile([P, J], U32, name="v_w", align_bytes=64)
-        v_s = keep.tile([P, J], U8, name="v_s", align_bytes=64)
+        v_s = keep.tile([P, EARLY], U8, name="v_s", align_bytes=64)
         whole, left, right = slice(0, J), slice(0, J // 2), slice(J // 2, J)
 
         def entries(cols):
@@ -92,10 +93,15 @@ def tile_list_hwayt_dl_tanh_kernel(
             )
             return codes[:].bitcast(FP8X4), scales[:]
 
+        def item_scales(cols):
+            if cols.stop <= EARLY:
+                return v_s[:, cols]
+            return v_s_late[:, cols.start - EARLY : cols.stop - EARLY]
+
         def product(acc, weights, cols, start, stop):
             nc.tensor.matmul_mx(
                 out=acc, lhsT=weights[0], lhsT_scale=weights[1],
-                rhs=v_w[:, cols].bitcast(FP8X4), rhs_scale=v_s[:, cols], start=start, stop=stop,
+                rhs=v_w[:, cols].bitcast(FP8X4), rhs_scale=item_scales(cols), start=start, stop=stop,
             )
 
         def wh4_half(h):
@@ -109,16 +115,24 @@ def tile_list_hwayt_dl_tanh_kernel(
         kept = [keep.tile([P, J], F32, name="kept%d" % h) for h in range(HALVES)]
         res = [keep.tile([P, J], F32, name="res%d" % h) for h in range(HALVES)]
 
-        def gate(h, weights, cols):
+        quarters = [slice(lo, lo + P) for lo in range(0, J, P)]
+        runs = [left, quarters[2], quarters[3]]
+
+        def group(acc, first_col, passes):
+            for n, (weights, cols) in enumerate(passes):
+                product(acc[:, cols.start - first_col : cols.stop - first_col], weights, cols, n == 0, n == len(passes) - 1)
+
+        def gate(h, weights, cols, pieces):
             ga = psum.tile([P, cols.stop - cols.start], F32, name="ga%d_%d" % (h, cols.start))
-            product(ga[:], weights, cols, True, True)
+            group(ga, cols.start, [(weights, piece) for piece in pieces])
             nc.scalar.activation(carry[h][:, cols], ga[:], ACT.Sigmoid, bias=neg_bias[:, h : h + 1], scale=-1.0)
 
-        def candidate(h, weights):
-            ha = psum.tile([P, J], F32, name="ha%d" % h)
-            product(ha[:], weights, whole, True, False)
-            product(ha[:], wh4_half(h), whole, False, True)
-            nc.scalar.activation(cand[h][:], ha[:], ACT.Tanh)
+        def candidate(h, weights, cols):
+            ha = psum.tile([P, cols.stop - cols.start], F32, name="ha%d_%d" % (h, cols.start))
+            change = [(weights, piece) for piece in runs if cols.start <= piece.start < cols.stop]
+            base = [(wh4_half(h), piece) for piece in quarters if cols.start <= piece.start < cols.stop]
+            group(ha, cols.start, change + base if h == 0 else base + change)
+            nc.scalar.activation(cand[h][:, cols], ha[:], ACT.Tanh)
 
         def keep_part(h, cols):
             nc.vector.tensor_tensor(kept[h][:, cols], r_rows[h][:].indirect(entries(cols)), carry[h][:, cols], ALU.mult)
@@ -133,25 +147,30 @@ def tile_list_hwayt_dl_tanh_kernel(
             nc.sync.dma_start(out[h * P : (h + 1) * P, cols], res[h][:, cols])
 
         gather_words(whole)
-        nc.vector.tensor_copy(v_s[:], tab_s[:].bitcast(U8).indirect(offsets[:]))
+        nc.vector.tensor_copy(v_s[:], tab_s[:].bitcast(U8).indirect(entries(slice(0, EARLY))))
         g0 = interleave(nc.scalar.copy, wg_raw, 0, "wg_g0", "wg_g0")
         g1 = interleave(nc.scalar.copy, wg_raw, 1, "wg_g1", "wg_g1")
         d1 = interleave(nc.scalar.copy, whd_raw, 1, "whd_g1", "whd_g1")
         nc.scalar.mul(neg_bias[:], bias[:], -1.0)
         wg0 = quantise(g0, "wg0", "wg0_codes")
+        v_s_late = keep.tile([P, J - EARLY], U8, name="v_s_late", tag="wg_raw", align_bytes=64)
+        nc.vector.tensor_copy(v_s_late[:], tab_s[:].bitcast(U8).indirect(entries(slice(EARLY, J))))
         wg1 = quantise(g1, "wg1", "wg1_codes")
         d0 = interleave(nc.vector.tensor_copy, whd_raw, 0, "whd_g0", "whd_g0")
         whd1 = quantise(d1, "whd1", "whd1_codes")
         whd0 = quantise(d0, "whd0", "whd0_codes")
-        first_pieces = [slice(0, J // 4), slice(J // 4, J // 2), right]
+        first_pieces = [quarters[0], slice(P, EARLY), quarters[3]]
         for cols in first_pieces:
-            gate(0, wg0, cols)
-        gate(1, wg1, whole)
-        candidate(0, whd0)
-        candidate(1, whd1)
+            gate(0, wg0, cols, [cols])
+        gate(1, wg1, left, runs[:1])
+        gate(1, wg1, right, runs[1:])
+        candidate(0, whd0, left)
+        candidate(0, whd0, right)
+        candidate(1, whd1, whole)
         for cols in first_pieces:
             keep_part(0, cols)
-        keep_part(1, whole)
+        keep_part(1, left)
+        keep_part(1, right)
         made = [keep.tile([P, J], F32, name="made%d" % h) for h in range(HALVES)]
         for h in range(HALVES):
             made_part(h, left)

@@ -142,9 +142,9 @@ def tile_list_hwayt_dl_tanh_kernel(
                 made[h][:, cols], carry[h][:, cols], -1.0, cand[h][:, cols], ALU.add, ALU.mult
             )
 
-        def finish(h, cols):
+        def finish(h, cols, queue):
             nc.vector.tensor_tensor(res[h][:, cols], kept[h][:, cols], made[h][:, cols], ALU.subtract)
-            nc.sync.dma_start(out[h * P : (h + 1) * P, cols], res[h][:, cols])
+            queue.dma_start(out[h * P : (h + 1) * P, cols], res[h][:, cols])
 
         gather_words(whole)
         nc.vector.tensor_copy(v_s[:], tab_s[:].bitcast(U8).indirect(entries(slice(0, EARLY))))
@@ -175,5 +175,8 @@ def tile_list_hwayt_dl_tanh_kernel(
         for h in range(HALVES):
             made_part(h, left)
             made_part(h, right)
-            finish(h, left)
-            finish(h, right)
+            if h == 0:
+                finish(h, left, nc.sync)
+                finish(h, right, nc.sync)
+        for n, cols in enumerate(quarters):
+            finish(1, cols, nc.sync if n % 2 else nc.scalar)

@@ -78,8 +78,8 @@ def tile_list_hwayt_dl_tanh_kernel(
         def interleave(engine_copy, raw, h, name, tag):
             grouped = keep.tile([P, P, PACK], BF16, name=name, tag=tag, align_bytes=64)
             engine_copy(
-                grouped[:].rearrange("p (c e) i -> p c i e", e=4),
-                raw[:, :, h * P : (h + 1) * P].rearrange("p i (c e) -> p c i e", e=4),
+                grouped[:].rearrange("p (c e) i -> p c i e", e=2),
+                raw[:, :, h * P : (h + 1) * P].rearrange("p i (c e) -> p c i e", e=2),
             )
             return grouped
 

@@ -169,8 +169,7 @@ def tile_list_hwayt_dl_tanh_kernel(
         candidate(1, whd1, whole)
         for cols in first_pieces:
             keep_part(0, cols)
-        keep_part(1, left)
-        keep_part(1, right)
+        keep_part(1, whole)
         made = [keep.tile([P, J], F32, name="made%d" % h) for h in range(HALVES)]
         for h in range(HALVES):
             made_part(h, left)

@@ -37,14 +37,19 @@ def tile_list_hwayt_dl_tanh_kernel(
         offsets = lists.tile([P, J // 16], U16, name="offsets")
         nc.sync.dma_start(offsets[:], offs)
 
-        def load_scale_rows(name, rows):
+        warm_in = keep.tile([P, 1], F32, name="warm_in")
+        warm_out = keep.tile([P, 1], F32, name="warm_out")
+        nc.vector.memset(warm_in[:], 0.0)
+        nc.scalar.activation(warm_out[:], warm_in[:], ACT.Sigmoid)
+
+        def load_scale_rows(name, rows, queues):
             plane = keep.tile([P, rows.shape[1]], I32, name=name, align_bytes=64)
             nc.vector.memset(plane[:], 0)
-            for q in range(4):
-                nc.sync.dma_start(plane[32 * q : 32 * q + 4, :], rows[4 * q : 4 * q + 4, :])
+            for q, queue in enumerate(queues):
+                queue.dma_start(plane[32 * q : 32 * q + 4, :], rows[4 * q : 4 * q + 4, :])
             return plane
 
-        tab_s = load_scale_rows("tab_s", tab_scales[0].bitcast(I32))
+        tab_s = load_scale_rows("tab_s", tab_scales[0].bitcast(I32), [nc.scalar, nc.sync, nc.scalar, nc.sync])
         wg_raw = keep.tile([P, PACK, N], F32, name="wg_raw", tag="wg_raw", align_bytes=64)
         nc.sync.dma_start(wg_raw[:], wg.rearrange("(p i) n -> p i n", i=PACK))
         whd_raw = keep.tile([P, PACK, N], F32, name="whd_raw", align_bytes=64)
@@ -54,15 +59,11 @@ def tile_list_hwayt_dl_tanh_kernel(
             nc.sync.dma_start(bias[:], bg.rearrange("(h p) -> p h", p=P))
         r_rows = [keep.tile([P, T], F32, name="r%d" % h, align_bytes=64) for h in range(HALVES)]
         nc.sync.dma_start(r_rows[0][:], rT[0:P, :])
-        wh4_s = load_scale_rows("wh4_s", wh4_scales[0].bitcast(I32))
+        wh4_s = load_scale_rows("wh4_s", wh4_scales[0].bitcast(I32), [nc.sync] * 4)
         nc.sync.dma_start(r_rows[1][:], rT[P : 2 * P, :])
         wh4_w = keep.tile([P, N // 2], I32, name="wh4_w", align_bytes=64)
         nc.sync.dma_start(wh4_w[:], wh4_words[0].bitcast(I32))
 
-        warm_in = keep.tile([P, 1], F32, name="warm_in")
-        warm_out = keep.tile([P, 1], F32, name="warm_out")
-        nc.vector.memset(warm_in[:], 0.0)
-        nc.scalar.activation(warm_out[:], warm_in[:], ACT.Sigmoid)
         neg_bias = keep.tile([P, HALVES], F32, name="neg_bias")
 
         v_w = keep.tile([P, J], U32, name="v_w", align_bytes=64)

from contextlib import ExitStack

import concourse.mybir as mybir

K, N, T, J = 512, 256, 1024, 512
FLOPS = 3 * 2 * K * N * J

F32 = mybir.dt.float32
BF16 = mybir.dt.bfloat16
I32 = mybir.dt.int32
U32 = mybir.dt.uint32
U16 = mybir.dt.uint16
U8 = mybir.dt.uint8
FP8X4 = mybir.dt.float8_e4m3fn_x4
FP4X4 = mybir.dt.float4_e2m1fn_x4
ALU = mybir.AluOpType
ACT = mybir.ActivationFunctionType

P = 128
PACK = 4
HALVES = N // P
EARLY = 384


def tile_list_hwayt_dl_tanh_kernel(
    tc, tab_words, tab_scales, wg, wh4_words, wh4_scales, whd, bg, rT, offs, out
):
    nc = tc.nc
    with ExitStack() as ctx:
        lists = ctx.enter_context(tc.tile_pool(name="lists", bufs=1))
        keep = ctx.enter_context(tc.tile_pool(name="keep", bufs=1))
        psum = ctx.enter_context(tc.psum_pool(name="psum", bufs=1))


        tab_w = keep.tile([P, T], I32, name="tab_w", align_bytes=64)
        nc.sync.dma_start(tab_w[:], tab_words[0].rearrange("p t i -> p (t i)").bitcast(I32))
        offsets = lists.tile([P, J // 16], U16, name="offsets")
        nc.sync.dma_start(offsets[:], offs)

        warm_in = keep.tile([P, 1], F32, name="warm_in")
        warm_out = keep.tile([P, 1], F32, name="warm_out")
        nc.vector.memset(warm_in[:], 0.0)
        nc.scalar.activation(warm_out[:], warm_in[:], ACT.Sigmoid)

        def load_scale_rows(name, rows, queues):
            plane = keep.tile([P, rows.shape[1]], I32, name=name, align_bytes=64)
            nc.vector.memset(plane[:], 0)
            for q, queue in enumerate(queues):
                queue.dma_start(plane[32 * q : 32 * q + 4, :], rows[4 * q : 4 * q + 4, :])
            return plane

        tab_s = load_scale_rows("tab_s", tab_scales[0].bitcast(I32), [nc.scalar, nc.sync, nc.scalar, nc.sync])
        wg_raw = keep.tile([P, PACK, N], F32, name="wg_raw", tag="wg_raw", align_bytes=64)
        nc.sync.dma_start(wg_raw[:], wg.rearrange("(p i) n -> p i n", i=PACK))
        whd_raw = keep.tile([P, PACK, N], F32, name="whd_raw", align_bytes=64)
        nc.sync.dma_start(whd_raw[:], whd.rearrange("(p i) n -> p i n", i=PACK))
        bias = keep.tile([P, HALVES], F32, name="bias")
        with nc.allow_non_contiguous_dma(reason="one bias value a partition"):
            nc.sync.dma_start(bias[:], bg.rearrange("(h p) -> p h", p=P))
        r_rows = [keep.tile([P, T], F32, name="r%d" % h, align_bytes=64) for h in range(HALVES)]
        nc.sync.dma_start(r_rows[0][:], rT[0:P, :])
        wh4_s = load_scale_rows("wh4_s", wh4_scales[0].bitcast(I32), [nc.sync] * 4)
        nc.sync.dma_start(r_rows[1][:], rT[P : 2 * P, :])
        wh4_w = keep.tile([P, N // 2], I32, name="wh4_w", align_bytes=64)
        nc.sync.dma_start(wh4_w[:], wh4_words[0].bitcast(I32))

        neg_bias = keep.tile([P, HALVES], F32, name="neg_bias")

        v_w = keep.tile([P, J], U32, name="v_w", align_bytes=64)
        v_s = keep.tile([P, EARLY], U8, name="v_s", align_bytes=64)
        whole, left, right = slice(0, J), slice(0, J // 2), slice(J // 2, J)

        def entries(cols):
            return offsets[:, cols.start // 16 : cols.stop // 16]

        def gather_words(cols):
            nc.vector.tensor_copy(v_w[:, cols], tab_w[:].bitcast(U32).indirect(entries(cols)))

        def interleave(engine_copy, raw, h, name, tag):
            grouped = keep.tile([P, P, PACK], BF16, name=name, tag=tag, align_bytes=64)
            engine_copy(
                grouped[:].rearrange("p (c e) i -> p c i e", e=2),
                raw[:, :, h * P : (h + 1) * P].rearrange("p i (c e) -> p c i e", e=2),
            )
            return grouped

        def quantise(grouped, name, tag):
            codes = keep.tile([P, P], U32, name=name + "_codes", tag=tag, align_bytes=64)
            scales = keep.tile([P, P], U8, name=name + "_scales", align_bytes=64)
            nc.vector.quantize_mx(
                out=codes[:].bitcast(FP8X4),
                scales=scales[:],
                in_=grouped[:].rearrange("p n i -> p (n i)"),
            )
            return codes[:].bitcast(FP8X4), scales[:]

        def item_scales(cols):
            if cols.stop <= EARLY:
                return v_s[:, cols]
            return v_s_late[:, cols.start - EARLY : cols.stop - EARLY]

        def product(acc, weights, cols, start, stop):
            nc.tensor.matmul_mx(
                out=acc, lhsT=weights[0], lhsT_scale=weights[1],
                rhs=v_w[:, cols].bitcast(FP8X4), rhs_scale=item_scales(cols), start=start, stop=stop,
            )

        def wh4_half(h):
            return (
                wh4_w[:].bitcast(U8)[:, 2 * h * P : 2 * (h + 1) * P].bitcast(FP4X4),
                wh4_s[:].bitcast(U8)[:, h * P : (h + 1) * P],
            )

        carry = [keep.tile([P, J], F32, name="carry%d" % h) for h in range(HALVES)]
        cand = [keep.tile([P, J], F32, name="cand%d" % h) for h in range(HALVES)]
        kept = [keep.tile([P, J], F32, name="kept%d" % h) for h in range(HALVES)]
        res = [keep.tile([P, J], F32, name="res%d" % h) for h in range(HALVES)]

        quarters = [slice(lo, lo + P) for lo in range(0, J, P)]
        runs = [left, quarters[2], quarters[3]]

        def group(acc, first_col, passes):
            for n, (weights, cols) in enumerate(passes):
                product(acc[:, cols.start - first_col : cols.stop - first_col], weights, cols, n == 0, n == len(passes) - 1)

        def gate(h, weights, cols, pieces):
            ga = psum.tile([P, cols.stop - cols.start], F32, name="ga%d_%d" % (h, cols.start))
            group(ga, cols.start, [(weights, piece) for piece in pieces])
            nc.scalar.activation(carry[h][:, cols], ga[:], ACT.Sigmoid, bias=neg_bias[:, h : h + 1], scale=-1.0)

        def candidate(h, weights, cols):
            ha = psum.tile([P, cols.stop - cols.start], F32, name="ha%d_%d" % (h, cols.start))
            change = [(weights, piece) for piece in runs if cols.start <= piece.start < cols.stop]
            base = [(wh4_half(h), piece) for piece in quarters if cols.start <= piece.start < cols.stop]
            group(ha, cols.start, change + base if h == 0 else base + change)
            nc.scalar.activation(cand[h][:, cols], ha[:], ACT.Tanh)

        def keep_part(h, cols):
            nc.vector.tensor_tensor(kept[h][:, cols], r_rows[h][:].indirect(entries(cols)), carry[h][:, cols], ALU.mult)

        def made_part(h, cols):
            nc.vector.scalar_tensor_tensor(
                made[h][:, cols], carry[h][:, cols], -1.0, cand[h][:, cols], ALU.add, ALU.mult
            )

        def finish(h, cols, queue):
            nc.vector.tensor_tensor(res[h][:, cols], kept[h][:, cols], made[h][:, cols], ALU.subtract)
            queue.dma_start(out[h * P : (h + 1) * P, cols], res[h][:, cols])

        gather_words(whole)
        nc.vector.tensor_copy(v_s[:], tab_s[:].bitcast(U8).indirect(entries(slice(0, EARLY))))
        g0 = interleave(nc.scalar.copy, wg_raw, 0, "wg_g0", "wg_g0")
        g1 = interleave(nc.scalar.copy, wg_raw, 1, "wg_g1", "wg_g1")
        d1 = interleave(nc.scalar.copy, whd_raw, 1, "whd_g1", "whd_g1")
        nc.scalar.mul(neg_bias[:], bias[:], -1.0)
        wg0 = quantise(g0, "wg0", "wg0_codes")
        v_s_late = keep.tile([P, J - EARLY], U8, name="v_s_late", tag="wg_raw", align_bytes=64)
        nc.vector.tensor_copy(v_s_late[:], tab_s[:].bitcast(U8).indirect(entries(slice(EARLY, J))))
        wg1 = quantise(g1, "wg1", "wg1_codes")
        d0 = interleave(nc.vector.tensor_copy, whd_raw, 0, "whd_g0", "whd_g0")
        whd1 = quantise(d1, "whd1", "whd1_codes")
        whd0 = quantise(d0, "whd0", "whd0_codes")
        first_pieces = [quarters[0], slice(P, EARLY), quarters[3]]
        for cols in first_pieces:
            gate(0, wg0, cols, [cols])
        gate(1, wg1, left, runs[:1])
        gate(1, wg1, right, runs[1:])
        candidate(0, whd0, left)
        candidate(0, whd0, right)
        candidate(1, whd1, whole)
        for cols in first_pieces:
            keep_part(0, cols)
        keep_part(1, whole)
        made = [keep.tile([P, J], F32, name="made%d" % h) for h in range(HALVES)]
        for h in range(HALVES):
            made_part(h, left)
            made_part(h, right)
            if h == 0:
                finish(h, left, nc.sync)
                finish(h, right, nc.sync)
        for n, cols in enumerate(quarters):
            finish(1, cols, nc.sync if n % 2 else nc.scalar)
